import numpy as np
import ml_dtypes


def mxq(x, axis, fmt="e4m3"):
    dtype, down = {"e4m3": (ml_dtypes.float8_e4m3fn, 7), "e5m2": (ml_dtypes.float8_e5m2, 14)}[fmt]
    v = np.moveaxis(np.asarray(x, np.float32).astype(ml_dtypes.bfloat16).astype(np.float64), axis, -1)
    blocks = v.reshape(v.shape[:-1] + (-1, 32))
    amax = np.abs(blocks).max(-1, keepdims=True)
    byte = np.maximum(np.where(amax > 0, np.frexp(amax)[1] - 1 + 127, 0) - down, 1)
    scale = np.exp2(byte - 127.0)
    codes = (blocks / scale).astype(np.float32).astype(dtype).astype(np.float64)
    return np.moveaxis((codes * scale).reshape(v.shape), -1, axis)


WIDE = False


def mx_kscale(k):
    if not WIDE:
        return np.ones(k)
    levels = np.array([10, -10, 5, -5, 0])
    if k % 512:
        return np.exp2(np.random.permutation(np.resize(levels, k // 32))).repeat(32)
    a = np.empty((k // 512, 16))
    for p in range(k // 512):
        a[p, :8] = np.random.permutation(np.resize(levels, 8))
        for g in range(8):
            far = levels[np.abs(levels - a[p, g]) >= 10]
            a[p, g + 8] = far[np.random.randint(len(far))]
    return np.exp2(a.ravel()).repeat(32)


def f64(x):
    return np.asarray(x).astype(np.float64)


def striped(idx):
    return np.tile(idx.reshape(-1, 16).T, (8, 1)).astype(np.uint16)


def unstriped(offs):
    return offs[:16].T.reshape(-1).astype(np.int64)


def striped8(idx):
    return np.concatenate([x.reshape(-1, 16).T for x in idx]).astype(np.uint16)


def runs(offs, k):
    lists = np.stack([offs[16 * r : 16 * r + 16].T.reshape(-1) for r in range(8)]).astype(np.int64)
    return lists[np.arange(k) % 512 // 64]


def pack_weight(w):
    k, n = w.shape
    w = f64(np.asarray(w, np.float32).astype(ml_dtypes.bfloat16)).reshape(k // 32, 32, n)
    amax = np.abs(w).max(1)
    byte = np.clip(np.where(amax > 0, np.frexp(amax)[1] - 1 + 127 - 7, 1), 1, 254)
    scaled = (w * np.exp2(127.0 - byte)[:, None, :]).reshape(k, n).astype(np.float32)
    words = np.ascontiguousarray(scaled.reshape(k // 512, 128, 4, n).transpose(0, 1, 3, 2)).astype(ml_dtypes.float8_e4m3fn).view(np.uint8)
    return words, np.ascontiguousarray(byte.astype(np.uint8).reshape(k // 512, 16, n))


def unpack_weight(words, scales):
    g, p, n, _ = words.shape
    vals = np.ascontiguousarray(words).view(ml_dtypes.float8_e4m3fn).astype(np.float64) * np.repeat(np.exp2(scales.astype(np.float64) - 127.0), 8, axis=1)[..., None]
    return vals.transpose(0, 1, 3, 2).reshape(g * 512, n)


def sigmoid(v):
    return 1.0 / (1.0 + np.exp(-np.maximum(v, -700.0)))


K, T, S, N, H = 512, 2048, 512, 512, 512


def setup_inputs():
    n = np.random.standard_normal
    s = mx_kscale(K)[:, None]
    u = mx_kscale(S)
    packed_xT = pack_weight(n((K, T)) * s)
    return {
        "x_words": packed_xT[0],
        "x_scales": packed_xT[1],
        "wa": (n((K, H)) / np.sqrt(K) / s).astype(np.float32),
        "wb": (n((K, N)) / np.sqrt(K) / s).astype(np.float32),
        "gt": (np.random.uniform(0.5, 1.5, (S, 1)) * u[:, None]).astype(np.float32),
        "gi": (np.random.uniform(0.5, 1.5, (S, 1)) / u[:, None]).astype(np.float32),
        "offs": striped(np.random.permutation(T)[:S]),
        "two": striped(np.random.permutation(T)[:S]),
        "fa": striped8(np.stack([np.random.permutation(H) for _ in range(8)])),
        "fb": striped8(np.stack([np.random.permutation(N) for _ in range(8)])),
    }


def reference(x_words, x_scales, wa, wb, gt, gi, offs, two, fa, fb):
    xq = unpack_weight(x_words, x_scales)[:, unstriped(offs)]
    a = xq.T @ mxq(f64(wa), 0, "e4m3")
    z = f64(gt) * (a * (sigmoid(a[np.arange(S)[:, None], runs(fa, S)])))
    x_two = unpack_weight(x_words, x_scales)[:, unstriped(two)]
    b = x_two.T @ mxq(f64(wb), 0, "e4m3")
    z2 = f64(gi) * (b * (sigmoid(b[np.arange(S)[:, None], runs(fb, S)])))
    cv = 0.0625 * ((mxq(z, 0, "e4m3").T @ mxq(z2, 0, "e4m3")))
    return np.tanh(cv)

@@ -1,0 +1,182 @@
+from contextlib import ExitStack
+
+import concourse.mybir as mybir
+
+K, T, S, H, N = 512, 2048, 512, 512, 512
+FLOPS = 2 * K * S * H + 2 * K * S * N + 2 * S * H * N
+
+F32 = mybir.dt.float32
+BF16 = mybir.dt.bfloat16
+I32 = mybir.dt.int32
+U32 = mybir.dt.uint32
+U16 = mybir.dt.uint16
+U8 = mybir.dt.uint8
+FP8X4 = mybir.dt.float8_e4m3fn_x4
+ACT = mybir.ActivationFunctionType
+MULT = mybir.AluOpType.mult
+
+P = 128
+PACK = 4
+HALF = 256
+QUARTER = 128
+RUN = 4
+HEAD = 256
+
+
+def tile_picked_momprod_none_p_kernel(
+    tc, x_words, x_scales, wa, wb, gt, gi, offs, two, fa, fb, out
+):
+    nc = tc.nc
+    with ExitStack() as ctx:
+        lists = ctx.enter_context(tc.tile_pool(name="lists", bufs=1))
+        keep = ctx.enter_context(tc.tile_pool(name="keep", bufs=1))
+        psum = ctx.enter_context(tc.psum_pool(name="psum", bufs=8))
+
+        def sbuf(name, shape, dtype, tag=None):
+            return keep.tile(shape, dtype, name=name, tag=tag or name, align_bytes=64)
+
+        def load_list(name, src):
+            tile = lists.tile([P, S // 16], U16, name=name)
+            nc.sync.dma_start(tile[:], src)
+            return tile
+
+        def load_weight_half(name, w, h):
+            raw = sbuf("%s_raw%d" % (name, h), [P, PACK, HALF], F32)
+            nc.sync.dma_start(raw[:], w.rearrange("(p j) c -> p j c", j=PACK)[:, :, h * HALF : (h + 1) * HALF])
+            return raw
+
+        def load_gain(name, g):
+            tile = sbuf(name, [P, PACK], F32)
+            nc.sync.dma_start(tile[:], g.rearrange("(p t) o -> p (t o)", t=PACK))
+            return tile
+
+        def interleave(copy, name, rows, width):
+            grouped = sbuf(name, [P, width, PACK], BF16)
+            copy(
+                grouped[:].rearrange("p (c i) t -> p c t i", i=RUN),
+                rows[:].rearrange("p t (c i) -> p c t i", i=RUN),
+            )
+            return grouped
+
+        def quantize(grouped, codes, scales):
+            nc.vector.quantize_mx(
+                out=codes.bitcast(FP8X4), scales=scales, in_=grouped[:].rearrange("p c t -> p (c t)")
+            )
+
+        def pick(name, table, offsets, dtype):
+            picked = sbuf(name, [P, S], dtype)
+            nc.vector.tensor_copy(picked[:].rearrange("p (t m) -> p m t", t=PACK), table[:].indirect(offsets[:]))
+            return picked
+
+        on_scalar, on_vector, on_gpsimd = nc.scalar.copy, nc.vector.tensor_copy, nc.gpsimd.tensor_copy
+
+        scale_table = sbuf("scale_table", [P, T], U8)
+        nc.vector.memset(scale_table[:].bitcast(I32), 0)
+        word_table = sbuf("word_table", [P, T], U32)
+        words_hbm = x_words[0].rearrange("p n t -> p (n t)").bitcast(I32)
+        nc.sync.dma_start(word_table[:, :HEAD].bitcast(I32), words_hbm[:, :HEAD])
+        two_t = load_list("two_t", two)
+        offs_t = load_list("offs_t", offs)
+        for q in range(4):
+            queue = nc.sync if q < 2 else nc.scalar
+            queue.dma_start(
+                scale_table[32 * q : 32 * q + 4, :].bitcast(I32), x_scales[0, 4 * q : 4 * q + 4, :].bitcast(I32)
+            )
+        nc.sync.dma_start(word_table[:, HEAD:].bitcast(I32), words_hbm[:, HEAD:])
+        wb_raw = [load_weight_half("wb", wb, h) for h in range(2)]
+        fb_t = load_list("fb_t", fb)
+        gi_t = load_gain("gi_t", gi)
+        wa_raw = [load_weight_half("wa", wa, h) for h in range(2)]
+        fa_t = load_list("fa_t", fa)
+        gt_t = load_gain("gt_t", gt)
+
+        def project(name, words, scales, raw, copies):
+            codes = sbuf(name + "_codes", [P, H], U32)
+            planes = sbuf(name + "_planes", [P, H], U8)
+            banks = [psum.tile([P, H], F32, name="bank") for t in range(PACK)]
+
+            def multiply(t, cols):
+                rows = slice(t * P, (t + 1) * P)
+                nc.tensor.matmul_mx(
+                    out=banks[t][:, cols],
+                    lhsT=words[:, rows].bitcast(FP8X4),
+                    lhsT_scale=scales[:, rows],
+                    rhs=codes[:, cols].bitcast(FP8X4),
+                    rhs_scale=planes[:, cols],
+                    start=True,
+                    stop=True,
+                )
+
+            for h in range(2):
+                cols = slice(h * HALF, (h + 1) * HALF)
+                grouped = interleave(copies[h], "%s_grouped%d" % (name, h), raw[h], HALF)
+                quantize(grouped, codes[:, cols], planes[:, cols])
+                multiply(0, cols)
+            for t in range(1, PACK):
+                multiply(t, slice(0, H))
+            return banks
+
+        def to_window(name, bank, copy):
+            window = sbuf(name, [P, H], F32)
+            copy(window[:], bank[:])
+            return window
+
+        def gate(name, window, offsets, c0, width):
+            g = sbuf(name, [P, width], F32)
+            nc.scalar.activation(g[:], window[:].indirect(offsets[:, c0 // 16 : (c0 + width) // 16]), ACT.Sigmoid)
+            return g
+
+        def gated_rows(name, banks, gain, gates, c0, width, tag=None):
+            rows = sbuf(name, [P, PACK, width], BF16, tag)
+            for t in range(PACK):
+                nc.vector.scalar_tensor_tensor(
+                    rows[:, t, :], banks[t][:, c0 : c0 + width], gain[:, t : t + 1], gates[t][:], MULT, MULT
+                )
+            return rows
+
+        b_scales = pick("b_scales", scale_table, two_t, U8)
+        a_scales = pick("a_scales", scale_table, offs_t, U8)
+        b_words = pick("b_words", word_table, two_t, U32)
+        a_words = pick("a_words", word_table, offs_t, U32)
+        b_banks = project("wb", b_words, b_scales, wb_raw, [on_scalar, on_scalar])
+        b_gates = [[], []]
+        b_copies = [on_vector, on_vector, on_vector, on_vector]
+        for t in range(PACK):
+            window = to_window("b_window%d" % t, b_banks[t], b_copies[t])
+            for h in range(2):
+                b_gates[h].append(gate("b_gate%d_%d" % (t, h), window, fb_t, h * HALF, HALF))
+        a_banks = project("wa", a_words, a_scales, wa_raw, [on_scalar, on_vector])
+        a_copies = [on_vector, on_scalar, on_vector, on_scalar]
+        a_windows = [to_window("a_window%d" % t, a_banks[t], a_copies[t]) for t in range(PACK)]
+        chunks = [(0, HALF), (HALF, QUARTER), (HALF + QUARTER, QUARTER)]
+        a_gates = [
+            [gate("a_gate%d_%d" % (t, c0), a_windows[t], fa_t, c0, width) for t in range(PACK)]
+            for c0, width in chunks
+        ]
+
+        z2_codes = sbuf("z2_codes", [P, N], U32)
+        z2_planes = sbuf("z2_planes", [P, N], U8)
+        for h in range(2):
+            cols = slice(h * HALF, (h + 1) * HALF)
+            rows = gated_rows("z2_rows%d" % h, b_banks, gi_t, b_gates[h], h * HALF, HALF, "wa_grouped%d" % h)
+            quantize(interleave(on_vector, "z2_grouped%d" % h, rows, HALF), z2_codes[:, cols], z2_planes[:, cols])
+
+        for (c0, width), gates in zip(chunks, a_gates):
+            rows = gated_rows("z_rows%d" % c0, a_banks, gt_t, gates, c0, width)
+            z_codes = sbuf("z_codes%d" % c0, [P, width], U32)
+            z_planes = sbuf("z_planes%d" % c0, [P, width], U8)
+            quantize(interleave(on_vector, "z_grouped%d" % c0, rows, width), z_codes[:], z_planes[:])
+            for m0 in range(0, width, P):
+                cv = psum.tile([P, N], F32, name="bank")
+                nc.tensor.matmul_mx(
+                    out=cv[:],
+                    lhsT=z_codes[:, m0 : m0 + P].bitcast(FP8X4),
+                    lhsT_scale=z_planes[:, m0 : m0 + P],
+                    rhs=z2_codes[:].bitcast(FP8X4),
+                    rhs_scale=z2_planes[:],
+                    start=True,
+                    stop=True,
+                )
+                result = sbuf("result%d" % (c0 + m0), [P, N], F32)
+                nc.scalar.activation(result[:], cv[:], ACT.Tanh, scale=0.0625)
+                nc.sync.dma_start(out[c0 + m0 : c0 + m0 + P, :], result[:])

@@ -70,6 +70,11 @@ def tile_picked_momprod_none_p_kernel(
 
         on_scalar, on_vector, on_gpsimd = nc.scalar.copy, nc.vector.tensor_copy, nc.gpsimd.tensor_copy
 
+        warm_in = sbuf("warm_in", [P, 1], F32)
+        warm_out = sbuf("warm_out", [P, 1], F32)
+        nc.gpsimd.memset(warm_in[:], 0.0)
+        nc.scalar.activation(warm_out[:], warm_in[:], ACT.Sigmoid)
+
         scale_table = sbuf("scale_table", [P, T], U8)
         nc.vector.memset(scale_table[:].bitcast(I32), 0)
         word_table = sbuf("word_table", [P, T], U32)

from contextlib import ExitStack

import concourse.mybir as mybir

K, T, S, H, N = 512, 2048, 512, 512, 512
FLOPS = 2 * K * S * H + 2 * K * S * N + 2 * S * H * N

F32 = mybir.dt.float32
BF16 = mybir.dt.bfloat16
I32 = mybir.dt.int32
U32 = mybir.dt.uint32
U16 = mybir.dt.uint16
U8 = mybir.dt.uint8
FP8X4 = mybir.dt.float8_e4m3fn_x4
ACT = mybir.ActivationFunctionType
MULT = mybir.AluOpType.mult

P = 128
PACK = 4
HALF = 256
QUARTER = 128
RUN = 4
HEAD = 256


def tile_picked_momprod_none_p_kernel(
    tc, x_words, x_scales, wa, wb, gt, gi, offs, two, fa, fb, out
):
    nc = tc.nc
    with ExitStack() as ctx:
        lists = ctx.enter_context(tc.tile_pool(name="lists", bufs=1))
        keep = ctx.enter_context(tc.tile_pool(name="keep", bufs=1))
        psum = ctx.enter_context(tc.psum_pool(name="psum", bufs=8))

        def sbuf(name, shape, dtype, tag=None):
            return keep.tile(shape, dtype, name=name, tag=tag or name, align_bytes=64)

        def load_list(name, src):
            tile = lists.tile([P, S // 16], U16, name=name)
            nc.sync.dma_start(tile[:], src)
            return tile

        def load_weight_half(name, w, h):
            raw = sbuf("%s_raw%d" % (name, h), [P, PACK, HALF], F32)
            nc.sync.dma_start(raw[:], w.rearrange("(p j) c -> p j c", j=PACK)[:, :, h * HALF : (h + 1) * HALF])
            return raw

        def load_gain(name, g):
            tile = sbuf(name, [P, PACK], F32)
            nc.sync.dma_start(tile[:], g.rearrange("(p t) o -> p (t o)", t=PACK))
            return tile

        def interleave(copy, name, rows, width):
            grouped = sbuf(name, [P, width, PACK], BF16)
            copy(
                grouped[:].rearrange("p (c i) t -> p c t i", i=RUN),
                rows[:].rearrange("p t (c i) -> p c t i", i=RUN),
            )
            return grouped

        def quantize(grouped, codes, scales):
            nc.vector.quantize_mx(
                out=codes.bitcast(FP8X4), scales=scales, in_=grouped[:].rearrange("p c t -> p (c t)")
            )

        def pick(name, table, offsets, dtype):
            picked = sbuf(name, [P, S], dtype)
            nc.vector.tensor_copy(picked[:].rearrange("p (t m) -> p m t", t=PACK), table[:].indirect(offsets[:]))
            return picked

        on_scalar, on_vector, on_gpsimd = nc.scalar.copy, nc.vector.tensor_copy, nc.gpsimd.tensor_copy

        warm_in = sbuf("warm_in", [P, 1], F32)
        warm_out = sbuf("warm_out", [P, 1], F32)
        nc.gpsimd.memset(warm_in[:], 0.0)
        nc.scalar.activation(warm_out[:], warm_in[:], ACT.Sigmoid)

        scale_table = sbuf("scale_table", [P, T], U8)
        nc.vector.memset(scale_table[:].bitcast(I32), 0)
        word_table = sbuf("word_table", [P, T], U32)
        words_hbm = x_words[0].rearrange("p n t -> p (n t)").bitcast(I32)
        nc.sync.dma_start(word_table[:, :HEAD].bitcast(I32), words_hbm[:, :HEAD])
        two_t = load_list("two_t", two)
        offs_t = load_list("offs_t", offs)
        for q in range(4):
            queue = nc.sync if q < 2 else nc.scalar
            queue.dma_start(
                scale_table[32 * q : 32 * q + 4, :].bitcast(I32), x_scales[0, 4 * q : 4 * q + 4, :].bitcast(I32)
            )
        nc.sync.dma_start(word_table[:, HEAD:].bitcast(I32), words_hbm[:, HEAD:])
        wb_raw = [load_weight_half("wb", wb, h) for h in range(2)]
        fb_t = load_list("fb_t", fb)
        gi_t = load_gain("gi_t", gi)
        wa_raw = [load_weight_half("wa", wa, h) for h in range(2)]
        fa_t = load_list("fa_t", fa)
        gt_t = load_gain("gt_t", gt)

        def project(name, words, scales, raw, copies):
            codes = sbuf(name + "_codes", [P, H], U32)
            planes = sbuf(name + "_planes", [P, H], U8)
            banks = [psum.tile([P, H], F32, name="bank") for t in range(PACK)]

            def multiply(t, cols):
                rows = slice(t * P, (t + 1) * P)
                nc.tensor.matmul_mx(
                    out=banks[t][:, cols],
                    lhsT=words[:, rows].bitcast(FP8X4),
                    lhsT_scale=scales[:, rows],
                    rhs=codes[:, cols].bitcast(FP8X4),
                    rhs_scale=planes[:, cols],
                    start=True,
                    stop=True,
                )

            for h in range(2):
                cols = slice(h * HALF, (h + 1) * HALF)
                grouped = interleave(copies[h], "%s_grouped%d" % (name, h), raw[h], HALF)
                quantize(grouped, codes[:, cols], planes[:, cols])
                multiply(0, cols)
            for t in range(1, PACK):
                multiply(t, slice(0, H))
            return banks

        def to_window(name, bank, copy):
            window = sbuf(name, [P, H], F32)
            copy(window[:], bank[:])
            return window

        def gate(name, window, offsets, c0, width):
            g = sbuf(name, [P, width], F32)
            nc.scalar.activation(g[:], window[:].indirect(offsets[:, c0 // 16 : (c0 + width) // 16]), ACT.Sigmoid)
            return g

        def gated_rows(name, banks, gain, gates, c0, width, tag=None):
            rows = sbuf(name, [P, PACK, width], BF16, tag)
            for t in range(PACK):
                nc.vector.scalar_tensor_tensor(
                    rows[:, t, :], banks[t][:, c0 : c0 + width], gain[:, t : t + 1], gates[t][:], MULT, MULT
                )
            return rows

        b_scales = pick("b_scales", scale_table, two_t, U8)
        a_scales = pick("a_scales", scale_table, offs_t, U8)
        b_words = pick("b_words", word_table, two_t, U32)
        a_words = pick("a_words", word_table, offs_t, U32)
        b_banks = project("wb", b_words, b_scales, wb_raw, [on_scalar, on_scalar])
        b_gates = [[], []]
        b_copies = [on_vector, on_vector, on_vector, on_vector]
        for t in range(PACK):
            window = to_window("b_window%d" % t, b_banks[t], b_copies[t])
            for h in range(2):
                b_gates[h].append(gate("b_gate%d_%d" % (t, h), window, fb_t, h * HALF, HALF))
        a_banks = project("wa", a_words, a_scales, wa_raw, [on_scalar, on_vector])
        a_copies = [on_vector, on_scalar, on_vector, on_scalar]
        a_windows = [to_window("a_window%d" % t, a_banks[t], a_copies[t]) for t in range(PACK)]
        chunks = [(0, HALF), (HALF, QUARTER), (HALF + QUARTER, QUARTER)]
        a_gates = [
            [gate("a_gate%d_%d" % (t, c0), a_windows[t], fa_t, c0, width) for t in range(PACK)]
            for c0, width in chunks
        ]

        z2_codes = sbuf("z2_codes", [P, N], U32)
        z2_planes = sbuf("z2_planes", [P, N], U8)
        for h in range(2):
            cols = slice(h * HALF, (h + 1) * HALF)
            rows = gated_rows("z2_rows%d" % h, b_banks, gi_t, b_gates[h], h * HALF, HALF, "wa_grouped%d" % h)
            quantize(interleave(on_vector, "z2_grouped%d" % h, rows, HALF), z2_codes[:, cols], z2_planes[:, cols])

        for (c0, width), gates in zip(chunks, a_gates):
            rows = gated_rows("z_rows%d" % c0, a_banks, gt_t, gates, c0, width)
            z_codes = sbuf("z_codes%d" % c0, [P, width], U32)
            z_planes = sbuf("z_planes%d" % c0, [P, width], U8)
            quantize(interleave(on_vector, "z_grouped%d" % c0, rows, width), z_codes[:], z_planes[:])
            for m0 in range(0, width, P):
                cv = psum.tile([P, N], F32, name="bank")
                nc.tensor.matmul_mx(
                    out=cv[:],
                    lhsT=z_codes[:, m0 : m0 + P].bitcast(FP8X4),
                    lhsT_scale=z_planes[:, m0 : m0 + P],
                    rhs=z2_codes[:].bitcast(FP8X4),
                    rhs_scale=z2_planes[:],
                    start=True,
                    stop=True,
                )
                result = sbuf("result%d" % (c0 + m0), [P, N], F32)
                nc.scalar.activation(result[:], cv[:], ACT.Tanh, scale=0.0625)
                nc.sync.dma_start(out[c0 + m0 : c0 + m0 + P, :], result[:])
